import numpy as np, ml_dtypes
CORES = [9,25,41,57]
N = 4
BF = ml_dtypes.bfloat16
A, W, HM, RO, MU = 512, 4096, 2, 5, 8
n = A // 4
def view(j, c):
    return np.where(c < 0, W, (((c * (MU * j + 5)) >> 5) + 37 * j) & (W - 1))
def worth(tab, j, b):
    x = tab[:, view(j[None, :], b)]
    return np.add.reduce(np.maximum.accumulate(x[:, ::-1], axis=1)[:, ::-1], axis=0)
def pack(x, b, p):
    return {"sight": x.reshape(N, 128, W).astype(np.float32).astype(BF), "bun": np.ascontiguousarray(b.reshape(N, 128, A)).astype(np.int32), "pots": p.astype(np.int32)}
def looks(rng):
    return (rng.integers(0, 256, (N, 8, 16, W)) * rng.integers(1, 9, (N, 8, 1, W))) >> 3
def some(rng, goods, shares):
    return np.where(rng.random((N, 8, 16, A)) < rng.choice(np.array(shares), (N, 8, 1, A)), goods, -1)
def setup_inputs(rng):
    b = some(rng, rng.integers(0, 4096, (N, 8, 16, A)), [0.05, 0.2, 0.4, 0.7, 1.0])
    p = np.where(rng.random((N, 8, n)) < 0.85, rng.integers(0, 4096, (N, 8, n)), -1)
    return pack(looks(rng), b, p)
def setup_inputs_spread(rng):
    x = np.floor(np.exp2(8 * rng.random((N, 8, 1, W)) * rng.random((N, 8, 16, W)) ** 0.5)).astype(np.int64) - 1
    x = np.where(rng.random((N, 8, 16, W)) < 0.02, 255, np.clip(x, 0, 255))
    e = rng.choice(np.array([0.5, 1.0, 3.0, 6.0]), (N, 8, 1, A))
    b = some(rng, np.minimum((4096 * rng.random((N, 8, 16, A)) ** e).astype(np.int64), 4095), [0.05, 0.15, 0.5, 0.95])
    p = np.minimum((4096 * rng.random((N, 8, n)) ** rng.choice(np.array([0.3, 1.0, 4.0]), (N, 8, 1))).astype(np.int64), 4095)
    return pack(x, b, np.where(rng.random((N, 8, n)) < 0.9, p, -1))
def setup_inputs_ends(rng):
    see = view(np.arange(A), np.int64(4095))
    x = 255 * (rng.random((N, 8, 16, W)) < rng.choice(np.array([0.05, 0.3, 0.6, 0.95]), (N, 8, 1, W))).astype(np.int64)
    x[:, :, 0, see[0::4]] = 255
    far = np.array([0, A - 67, A - 66, A - 65, A - 4, A - 3, A - 2, A - 1]); x[..., see[far]] = 255
    b = some(rng, np.int64(4095), [0.0, 0.1, 0.5, 1.0])
    own = (rng.random((N, 8, 1, A)) < 0.33) & (np.arange(A) % 4 != 0)
    b = np.where(own, rng.integers(0, 4096, (N, 8, 16, A)), b)
    b[:, :, 3, 0::4] = 4095; b[..., 0] = 4095; b[..., A - 67:A - 64] = -1; b[..., A - 4] = -1
    end = np.where(rng.random((N, 8, 1, 3)) < 0.5, 4095, -1); end[N - 1, 7] = np.array([-1, 4095, -1]); end[0, 7] = np.array([-1, -1, 4095]); end[1, 7] = np.array([4095, -1, -1])
    b[..., A - 3:] = end
    p = np.where(rng.random((N, 8, n)) < 0.7, np.where(rng.random((N, 8, n)) < 0.6, 4095, -1), rng.integers(0, 4096, (N, 8, n)))
    p[..., 0] = 4095; p[..., n - 1] = 4095
    return pack(x, b, p)
def setup_inputs_corners(rng):
    x = looks(rng); b = rng.integers(0, 4096, (N, 8, 16, A)); p = rng.integers(0, 4096, (N, 8, n)); d = np.arange(16)[:, None]
    for r in range(N):
        mode = rng.permutation(8)
        for g in range(8):
            m = int(mode[g])
            if m == 0: b[r, g] = -1
            if m == 2: b[r, g, :15] = -1
            if m == 3: b[r, g, 1:] = -1
            if m == 4:
                c = int(b[r, g, 0, 0]); b[r, g] = np.where(rng.random((16, A)) < rng.random((1, A)), c, -1); p[r, g] = c
            if m == 5: b[r, g] = np.where(rng.random((1, A)) < 0.5, b[r, g], -1)
            if m == 6:
                k = rng.choice(np.array([0, 1, 15, 16]), (1, A)); low = rng.random((1, A)) < 0.5
                b[r, g] = np.where(np.where(low, d < k, d >= 16 - k), b[r, g], -1); p[r, g] = -1
            if m == 7: x[r, g] = 0
    return pack(x, b, p)
def calls(rng):
    return np.argsort(rng.random((N, 3, n)), axis=-1) + n * rng.integers(0, W // n, (N, 3, n))
def setup_inputs_ties(rng):
    base = rng.choice(np.array([0, 1, 127, 254]), (N, 8, 1, 1)); base[0, 0] = 0; base[0, 7] = 254; base[N - 1, 7] = 254
    x = base + (rng.random((N, 8, 16, W)) < 0.125)
    few = rng.integers(0, 4096, 32); few[0] = 0; few[1] = 4095
    b = some(rng, few[rng.integers(0, 32, (N, 8, 16, A))], [0.0, 0.1, 0.3, 0.6])
    p = np.where(rng.random((N, 8, n)) < 0.9, few[rng.integers(0, 32, (N, 8, n))], -1)
    full = rng.integers(0, 4096, (N, 16, A)); b3 = np.where(rng.random((N, 1, A)) < 0.5, full, -1)
    b3[:, :, 0::4] = full[:, :, 0::4]
    b3[:, 0:3, 0::4] = calls(rng)
    x[:, 3] = 100; b[:, 3] = b3
    for m in range(3):
        bm = rng.integers(0, 4096, (N, 16, A)); bm[:, 0:3, 0::4] = calls(rng); bm[:, :, m + 1::4] = -1
        x[:, 4 + m] = 100; b[:, 4 + m] = bm
    return pack(x, b, p)
def check_inputs(d):
    bad = []
    for k, lo, hi in (("sight", 0, 255), ("bun", -1, 4095), ("pots", -1, 4095)):
        v = np.asarray(d[k]).astype(np.float64)
        if not np.all((v >= lo) & (v <= hi) & (v == np.floor(v))): bad.append("range of " + k)
    return bad
def reference(sight, bun, pots):
    tab = np.zeros((N, 8, 16, W + 1), np.int32); tab[..., :W] = sight.astype(np.float32).reshape(N, 8, 16, W).astype(np.int32)
    bn = bun.astype(np.int64).reshape(N, 8, 16, A); p = pots.astype(np.int64); val = np.zeros((N, 8, A), np.int64)
    for r in range(N):
        for g in range(8): val[r, g] = worth(tab[r, g], np.arange(A), bn[r, g])[0]
    place = np.arange(16)[:, None]
    for t in range(RO):
        u = 4 * np.arange(n) + (t & 3); nbn = bn.copy(); nval = val.copy(); npots = np.zeros((N, 8, n), np.int64)
        for r in range(N):
            for g in range(8):
                old = bn[r, g][:, u]; s = old.copy(); s[15] = p[r, g]
                best = np.zeros(n, np.int64); who = np.full(n, -1); riv = []
                for m in range(3):
                    q = r if m < HM else (r + 1 + (t + m - HM) % (N - 1)) % N
                    j = 4 * ((old[m] + val[r, g, u] + 13 * t) & (n - 1)) + ((t + 1 + m) & 3)
                    first = np.zeros(n, bool); first[np.unique(j, return_index=True)[1]] = True
                    sv = worth(tab[q, g], j, s)
                    e = np.where(first, np.add.reduce((sv > val[q, g, j]).astype(np.int64), axis=0), 0)
                    who = np.where(e > best, m, who); best = np.maximum(best, e); riv.append((q, j, sv))
                new = s.copy()
                for m in range(3):
                    q, j, sv = riv[m]; c = np.flatnonzero(who == m); jc = j[c]
                    nbn[q, g][:, jc] = np.where(place >= best[c] - 1, s[:, c], -1); nval[q, g, jc] = sv[best[c] - 1, c]
                    new[:, c] = bn[q, g][:, jc]
                nbn[r, g][:, u] = new; nval[r, g, u] = worth(tab[r, g], u, new)[0]
                npots[(r + 1) % N, g] = np.where(best >= 2, s[np.maximum(best - 2, 0), np.arange(n)], old[15])
        bn, val, p = nbn, nval, npots
    return {"yb": bn.reshape(N, 128, A).astype(np.float32), "yv": val.astype(np.float32), "yp": p.astype(np.float32)}

import math
from concourse.bass import DstId, RemoteDMATransfer
from concourse.mybir import AluOpType as OP, ActivationFunctionType as AF

F, H, I, U = "float32", "bfloat16", "int32", "uint16"
RO = 5
CYC, PEC, WAKE, ISSUE, LAT, GAT, SCA, SLACK, VLATE = 0.001, 0.0008, 0.08, 1.2, 2.0, 1.6, 4.0, 0.1, 0.3
CHS = {"S": 4, "0": 4, "1": 4, "2": 4}

SCRATCH = {}


def _sb(name, w, d):
    SCRATCH[name] = ("sbuf", [128, w], d)


_sb("TAB", 4112, H)
_sb("RAWB", 512, I)
_sb("POTI", 128, I)
_sb("BF", 512, F)
_sb("WIN", 896, F)
_sb("VR", 896, F)
_sb("NU", 128, F)
for _m in ("0", "1", "2", "S"):
    _sb("OFF" + _m, 128, U)
    _sb("XI" + _m, 128, I)
    _sb("XJ" + _m, 128, I)
_sb("X01", 4096, H)
_sb("X2", 4096, H)
_sb("XS", 2048, H)
_sb("RST", 2048, H)
_sb("S2", 128, F)
_sb("SI", 128, F)
_sb("S1", 128, F)
_sb("S21", 256, F)
_sb("KS", 128, F)
_sb("KT", 128, I)
_sb("KI", 128, I)
_sb("KB", 128, H)
_sb("KB2", 128, H)
_sb("KRB", 384, H)
_sb("KM", 384, H)
_sb("LF", 24, F)
_sb("VL", 24, U)
_sb("ZB", 16, F)
_sb("ZC", 64, F)
_sb("VJ", 384, F)
_sb("EB", 3072, H)
_sb("NF", 384, H)
_sb("CM", 384, H)
_sb("CN", 384, H)
_sb("Z", 32, F)
_sb("ZN", 8, F)
_sb("ZQ", 8, F)
_sb("ZX", 128, H)
_sb("ZM", 128, F)
_sb("ZI", 40, I)
for _m in ("", "b"):
    _sb("LX" + _m, 8, U)
    _sb("NV" + _m, 128, F)
    _sb("NX" + _m, 128, H)
_sb("LST", 8, U)
_sb("PP", 128, F)
_sb("D3", 8, F)
_sb("LST2", 8, U)
_sb("OUTB", 512, F)
_sb("OUTV", 512, F)
_sb("OUTP", 128, F)
_sb("SM", RO * 256, F)
_sb("LM", RO * 256, F)
_sb("ZS", RO * 8, F)
_sb("ZL", RO * 8, F)
_sb("CS", (RO + 1) * 128, F)
_sb("WS", RO * 144, F)
_sb("WL", RO * 144, F)
_sb("PS", RO * 128, F)
_sb("PL", (RO + 1) * 128, F)
_sb("PQ", (RO + 1) * 128, F)
_sb("LS", RO * 8, F)
_sb("LQ", RO * 8, F)
_sb("II", 8, I)
_sb("RO8", 24, F)
_sb("EC", 24, F)
_sb("W8", 8, F)
_sb("COL", 32, F)
_sb("FF", 128, F)
_sb("FX", 128, F)
_sb("FG", 128, F)
_sb("FY", 128, F)
_sb("EXL", 8, U)
_sb("IDN", 128, H)
_sb("BO", 128, H)
_sb("MSK", 128, F)
_sb("BLK", 8, F)
_sb("GS", 8, H)
_sb("NSEL", 8, H)
_sb("SEL", 384, H)
_sb("S32", 384, H)
_sb("S148", 384, H)
_sb("EQ", 512, H)
_sb("EW", 512, H)
_sb("QS", 24, H)
_sb("DIF", 128, F)
_sb("TMP", 128, F)
_sb("PSEL", 128, F)
_sb("POLD", 128, F)
_sb("REV", 128, F)
_sb("NEGV", 128, F)
_sb("BIGN", 128, H)
_sb("BIAS", 128, H)
_sb("WT", 1024, H)
_sb("TH", 128, F)
_sb("AC", 512, F)
_sb("WC", 512, I)
_sb("IL", 8, F)
_sb("CX", 8, F)
for _m in range(8):
    SCRATCH["b%d" % _m] = ("psum", [128, 512], F)

SEMAPHORES = ["cv", "cs", "ct", "cg", "snd", "l0", "l1", "l2", "o0", "o1", "o2"]
for _m in range(RO + 1):
    SEMAPHORES += [_k + "%d" % _m for _k in "mkzcwpqf"]
TWO = (H, U)


def rank_program(g, core, T, topo):
    rank = T.rank_of(core)
    if rank is None:
        return
    N = len(T.cores)
    Q = {"v": g.vector, "s": g.scalar, "t": g.tensor, "g": g, "y": g.sync}
    ops = []
    acc = {}
    cnt, clk = {}, {}
    known = {e: {} for e in Q}

    def psum(n):
        return n[0] == "b" and len(n) == 2

    def op(eng, outs, ins, call, cost, kind="c", sem=None, inc=1, extra=()):
        k = len(ops)
        pre = {}
        for j in extra:
            pre[j] = False
        for wr, lst in ((True, outs), (False, ins)):
            for (_, n, lo, hi) in lst:
                for (alo, ahi, aw, ae, j) in acc.get(n, []):
                    if psum(n) and ae == "t" and eng == "t":
                        pre.setdefault(j, False)
                    elif (psum(n) and ae != eng) or (alo < hi and lo < ahi and (aw or wr)):
                        pre[j] = True
        for wr, lst in ((False, ins), (True, outs)):
            for (_, n, lo, hi) in lst:
                a = acc.setdefault(n, [])
                if psum(n) and eng == "t":
                    a[:] = [x for x in a if x[3] == eng]
                if wr:
                    a[:] = [x for x in a if not (lo <= x[0] and x[1] <= hi)]
                a.append((lo, hi, wr, eng, k))
        ops.append({"eng": eng, "call": call, "cost": cost, "pre": pre, "kind": kind, "sem": sem, "inc": inc,
                    "nm": (outs or ins)[0][1] + ("" if outs else "!")})
        return k

    def learn(eng, tk):
        Q[eng].wait_ge(T.sem[tk[0]], tk[1])
        for s, v in clk[tk].items():
            if known[eng].get(s, 0) < v:
                known[eng][s] = v

    def need(eng, toks):
        toks = sorted(toks)
        for tk in toks:
            if known[eng].get(tk[0], 0) >= tk[1]:
                continue
            if any(o != tk and clk[o].get(tk[0], 0) >= tk[1] and known[eng].get(o[0], 0) < o[1] for o in toks):
                continue
            learn(eng, tk)
        for tk in toks:
            if known[eng].get(tk[0], 0) < tk[1]:
                learn(eng, tk)

    def flush():
        n = len(ops)
        succ = [[] for _ in ops]
        left = [len(o["pre"]) for o in ops]
        for k, o in enumerate(ops):
            for j in o["pre"]:
                succ[j].append(k)
        prio = [0.0] * n
        for k in range(n - 1, -1, -1):
            prio[k] = ops[k]["cost"] + max([prio[j] + (WAKE if ops[j]["pre"][k] else 0.0) for j in succ[k]], default=0.0)
        free = {e: 0.0 for e in Q}
        free["r"] = 0.0
        ready = {k: 0.0 for k in range(n) if left[k] == 0}
        done = [0.0] * n
        seq = []
        while ready:
            cand = []
            for k, av in ready.items():
                for e in ops[k]["eng"]:
                    b = VLATE if len(ops[k]["eng"]) > 1 and e == "v" else 0.0
                    cand.append((max(free[e], av) + b if e != "r" else av, -prio[k], k, e))
            m0 = min(cand)[0] + SLACK
            st, _, k, e = min((x for x in cand if x[0] <= m0), key=lambda x: (x[1], x[0]))
            o = ops[k]
            st = max(free[e], ready[k]) if e != "r" else ready[k]
            del ready[k]
            o["on"], o["st"] = e, st
            if o["kind"] == "arr":
                done[k] = st
            elif o["kind"] == "dma":
                free[e] = st + 0.1
                done[k] = st + o["cost"]
            elif o["kind"] == "rem":
                free[e] = st + ISSUE
                done[k] = st + ISSUE + LAT
            else:
                done[k] = free[e] = st + o["cost"]
            seq.append(k)
            for j in succ[k]:
                left[j] -= 1
                if left[j] == 0:
                    ready[j] = max(done[i] + (WAKE if ops[j]["pre"][i] else 0.0) for i in ops[j]["pre"])
        tok = {}
        for k in seq:
            o = ops[k]
            e = o["on"]
            if o["kind"] == "arr":
                tok[k] = (o["sem"], o["inc"])
                clk[tok[k]] = {o["sem"]: o["inc"]}
                continue
            need(e, set(tok[j] for j, w in o["pre"].items() if w))
            if o["kind"] == "rem":
                o["call"]()
                continue
            sem = o["sem"] or "c" + e
            cnt[sem] = cnt.get(sem, 0) + o["inc"]
            tok[k] = (sem, cnt[sem])
            o["call"](e).then_inc(T.sem[sem], o["inc"])
            c = dict(known[e])
            c[sem] = cnt[sem]
            clk[tok[k]] = c
        return seq

    sent = [0]
    sends = {}

    def arrive(n, lo, hi, key, val):
        op("r", [(None, n, lo, hi)], [], None, 0.0, "arr", key, val, [sends[key]])

    def B(n, lo=0, hi=None):
        return (T[n][:, lo:SCRATCH[n][1][1] if hi is None else hi], n, lo, SCRATCH[n][1][1] if hi is None else hi)

    V, S_, P_ = g.vector, g.scalar, g.tensor

    def a_(x):
        return x[0] if isinstance(x, tuple) else x

    def cols(*xs):
        return [x for x in xs if isinstance(x, tuple)]

    def el(o, *xs):
        n = 1
        for d in o[0].shape[1:]:
            n *= d
        if all(SCRATCH[x[1]][2] in TWO for x in (o,) + xs):
            n = n // 2
        return max(64, n) * CYC

    def copy(o, i):
        return op("v", [o], [i], lambda e: V.tensor_copy(o[0], i[0]), el(o, i))

    def tt(o, x, y, f):
        c = el(o) if psum(x[1]) or psum(y[1]) or el(o) < 0.07 else 2 * el(o)
        return op("v", [o], [x, y], lambda e: V.tensor_tensor(o[0], x[0], y[0], f), c)

    def ts(o, x, s1, f1, s2=None, f2=None):
        if f2 is None:
            return op("v", [o], [x] + cols(s1), lambda e: V.tensor_scalar(o[0], x[0], a_(s1), None, f1), el(o, x))
        return op("v", [o], [x] + cols(s1, s2), lambda e: V.tensor_scalar(o[0], x[0], a_(s1), a_(s2), f1, f2), el(o, x))

    def scaled(o, x, c):
        return op("vs", [o], [x, c], lambda e: V.tensor_scalar(o[0], x[0], c[0], None, OP.mult) if e == "v"
                  else S_.activation(o[0], x[0], AF.Copy, scale=c[0]), el(o))

    def fill(o, c):
        return op("v", [o], [], lambda e: V.memset(o[0], c), el(o))

    def scan(o, d0, d1, f0, f1):
        return op("v", [o], [d0, d1], lambda e: V.tensor_tensor_scan(o[0], d0[0], d1[0], 0.0, f0, f1), el(o, d0, d1))

    def act(o, i, func=AF.Copy, scale=1.0, bias=0.0):
        if isinstance(bias, float) and bias == 0.0:
            return op("s", [o], [i] + cols(scale), lambda e: S_.activation(o[0], i[0], func, scale=a_(scale)), el(o))
        return op("s", [o], [i] + cols(bias, scale), lambda e: S_.activation(o[0], i[0], func, bias=a_(bias), scale=a_(scale)), el(o))

    def mm(o, l, r, start=True, stop=True):
        n = max(min(64, l[0].shape[1]), r[0].shape[1])
        return op("t", [o], [l, r], lambda e: P_.matmul(o[0], l[0], r[0], start, stop), n * PEC * (4 if SCRATCH[l[1]][2] == F else 1))

    def ind(w, off):
        return w[0].indirect(off[0])

    def gat(eng, o, w, off):
        return op(eng, [o], [w, off], lambda e: V.tensor_copy(o[0], ind(w, off)) if e == "v"
                  else S_.activation(o[0], ind(w, off), AF.Copy), 0.06 + 16 * off[0].shape[1] * CYC * GAT)

    def sca(w, off, i):
        return op("v", [w], [i, off], lambda e: V.tensor_copy(ind(w, off), i[0]), 0.06 + 128 * CYC * SCA)

    def scamul(w, off, x, y):
        return op("v", [w], [x, y, off], lambda e: V.tensor_tensor(ind(w, off), x[0], y[0], OP.mult), 0.06 + 128 * CYC * SCA)

    def iota(o, pattern, base, cm):
        c = 0.13 + 2 * el(o)
        if SCRATCH[o[1]][2] == I:
            return op("g", [o], [], lambda e: g.iota(o[0], pattern, base, cm), c)
        return op("g", [o], [], lambda e: g.iota(o[0], pattern, base, cm, allow_small_or_imprecise_dtypes=True), c)

    def dma(q, outs, ins, out, in_, sem):
        return op(q, outs, ins, lambda e: Q[q].dma_start(out, in_), 7.0 if sem == "l1" else 2.5, "dma", sem, 16)

    def addr(r):
        return topo.addr(T.cores[r])[:2]

    def send(r, dst, src, sem):
        m = topo.mask(core, T.cores[r])
        rid, pid = addr(r)
        sends[sem] = op("g", [], [src], lambda: g.remote_dma(dst[0], src[0], T.sem[sem], T.sem["snd"], pid, rid, m), ISSUE + LAT, "rem")
        sent[0] += len(topo.engines(core, T.cores[r]))

    def width(r):
        return len(topo.engines(T.cores[r], core))

    def col(k):
        return B("COL", k, k + 1)

    def cls(n, c):
        return B(n, 128 + 128 * c, 256 + 128 * c)

    def third(n, m):
        return B(n, 128 * m, 128 * m + 128)

    def eight(n, m):
        return B(n, 8 * m, 8 * m + 8)

    dma("y", [B("RAWB")], [], T.RAWB[:], T.bun[:], "l0")
    dma("y", [B("TAB", 0, 4096)], [], T.TAB[:, 0:4096], T.sight[:], "l1")
    fill(B("POTI"), 0)
    dma("y", [B("POTI")], [], T.POTI[0:128:16, :], T.pots[:], "l2")
    fill(B("TAB", 4096, 4112), 0.0)

    iota(B("II", 0, 1), [[1, 1]], 0, 1)
    iota(B("FX"), [[0, 8], [1, 16]], 0, 0)
    iota(B("FG"), [[1, 8], [0, 16]], 0, 0)
    iota(B("AC"), [[8, 4], [32, 128]], 5, 0)
    iota(B("WC"), [[37, 4], [148, 128]], 0, 0)
    iota(B("FF"), [[1, 128]], 0, 0)
    iota(B("RO8", 0, 3), [[-1, 3]], 15, 0)
    iota(B("RO8", 8, 12), [[8, 4]], 5, 0)
    iota(B("RO8", 12, 16), [[37, 4]], 0, 0)
    iota(B("RO8", 16, 24), [[16, 8]], 0, 0)
    iota(B("FY"), [[0, 8], [1, 16]], 1, 0)
    for c in range(4):
        z0, z1 = (2048 * (2 - m) + 128 + 128 * ((c + 1 + m) & 3) for m in range(2))
        iota(B("ZC", 16 * c, 16 * c + 16), [[z1 - z0, 2], [0, 8]], z0, 0)
    copy(col(0), B("II", 0, 1))
    ts(B("II", 1, 2), B("II", 0, 1), 15, OP.bitwise_and)
    ts(B("II", 2, 3), B("II", 0, 1), 4, OP.logical_shift_right)
    copy(B("COL", 1, 3), B("II", 1, 3))
    ts(B("BO"), B("FG"), col(2), OP.is_equal)
    ts(col(12), col(1), -1.0, OP.mult, 15.0, OP.add)
    ts(B("TMP"), B("FX"), col(12), OP.is_equal)
    tt(B("REV"), B("BO"), B("TMP"), OP.mult)
    for c in range(4):
        copy(third("BF", c), (T.RAWB[:, c::4], "RAWB", 0, 512))
        mm(third("b0", c), B("REV"), third("BF", c))
        act(cls("WIN", c), third("b0", c), AF.Identity, 1.0, 1.0)
    ts(B("WC"), B("WC"), 4095, OP.bitwise_and)
    fill(B("RST"), 1.0)
    op("v", [B("RST")], [], lambda e: V.memset(T.RST[:, 0:2048:16], 0.0), 128 * CYC)
    ts(B("IDN"), B("FF"), col(0), OP.is_equal)
    ts(B("MSK"), B("FX"), col(1), OP.is_equal)
    ts(B("BLK"), B("FF", 0, 8), col(2), OP.is_equal)
    copy(B("GS"), B("BLK"))
    copy(B("EXL"), B("FF", 0, 8))
    ts(col(3), col(1), 0.0, OP.is_equal)
    ts(col(4), col(1), 0.0, OP.is_gt)
    ts(col(8), col(1), 13.0, OP.is_ge)
    ts(col(9), col(1), -2.0, OP.mult, 18.0, OP.add)
    ts(col(10), col(0), 768.0, OP.add, 1.0 / 4096, OP.mult)
    ts(col(11), col(0), 3.0 * 2048 + 640 - 65536, OP.add, 1.0 / 4096, OP.mult)
    ts(B("ZC"), B("ZC"), 1.0 / 4096, OP.mult)
    ts(B("EC", 0, 3), B("RO8", 0, 3), col(1), OP.is_equal)
    ts(B("EC", 3, 6), B("EC", 0, 3), 32.0, OP.mult)
    ts(B("EC", 6, 9), B("EC", 0, 3), 148.0, OP.mult)
    ts(B("EC", 9, 17), B("RO8", 8, 16), col(3), OP.mult)
    ts(B("BIAS"), B("MSK"), 512.0, OP.mult, -512.0, OP.add)
    for m in range(3):
        scaled(third("SEL", m), B("BO"), B("EC", m, m + 1))
        scaled(third("S32", m), B("BO"), B("EC", 3 + m, 4 + m))
        scaled(third("S148", m), B("BO"), B("EC", 6 + m, 7 + m))
        ts(eight("QS", m), B("GS"), B("EC", m, m + 1), OP.mult, 1.0 / 4096, OP.mult)
    for c in range(4):
        scaled(third("EQ", c), B("BO"), B("EC", 9 + c, 10 + c))
        scaled(third("EW", c), B("BO"), B("EC", 13 + c, 14 + c))
    ts(B("IL"), B("RO8", 16, 24), col(1), OP.add)
    ts(B("CX"), B("IL"), 16.0, OP.mult, 4096.0 + 16.0, OP.add)
    fill(col(14), 63 * math.log(2.0))
    fill(col(15), 63 * math.log(2.0) + math.log(2.5))
    act(B("W8"), B("IL"), AF.Exp, -math.log(2.0), col(14))
    act(B("TH"), B("FF"), AF.Exp, -math.log(2.0), col(15))
    for c in range(8):
        scaled(third("WT", c), B("BO"), B("W8", c, c + 1))
    ts(B("NEGV"), B("BO"), col(3), OP.mult, -1.0, OP.mult)
    ts(B("BIGN"), B("BO"), col(3), OP.mult, -16384.0, OP.mult)
    ts(B("NSEL"), B("GS"), col(3), OP.mult, -64.0, OP.mult)
    fill(B("VR", 0, 128), 0.0)
    fill(B("VR", 640, 896), 0.0)
    fill(B("WIN", 0, 128), 0.0)
    ts(third("PL", 0), B("POTI"), 1.0, OP.add, col(3), OP.mult)
    ts(B("TMP"), B("FX"), 0.0, OP.is_equal)
    tt(B("PSEL"), B("BO"), B("TMP"), OP.mult)
    ts(col(16), col(1), 1.0, OP.is_equal)
    ts(B("POLD"), B("PSEL"), col(16), OP.mult)
    ts(col(13), col(3), 16.0, OP.mult, col(1), OP.add)
    ts(B("FY"), B("FY"), col(13), OP.is_equal)
    tt(B("TMP"), B("FY"), B("MSK"), OP.subtract)
    tt(B("DIF"), B("TMP"), B("BO"), OP.mult)
    ts(B("TMP"), B("FX"), 0.0, OP.is_gt)
    tt(B("DIF"), B("DIF"), B("TMP"), OP.mult)

    FLAG = (1 << 19) | 4095

    def index(tag, s, a, w):
        xi, xj, off = B("XI" + tag), B("XJ" + tag), B("OFF" + tag)
        tt(xi, s, a, OP.mult)
        ts(xj, xi, 5, OP.arith_shift_right, FLAG, OP.bitwise_and)
        tt(xi, xj, w, OP.add)
        ts(xj, xi, FLAG, OP.bitwise_and)
        ts(off, xj, 4096.0, OP.min)

    TABW = B("TAB", 0, 4097)

    def look(tag, xn, base):
        w = 128 // CHS[tag]
        for a in range(0, 128, w):
            x = B(xn, base + 16 * a, base + 16 * (a + w))
            gat("sv", x, TABW, B("OFF" + tag, a, a + w))
            scan(x, B("RST", 0, 16 * w), x, OP.mult, OP.max)

    def selfsum(xn, base, c, bank):
        o = B(bank, 128, 256)
        mm(o, B("BO"), (T[xn][:, base + 15:base + 2048:16], xn, base, base + 2048))
        act(cls("VR", c), o)

    for c, (tag, xn, base) in enumerate((("S", "XS", 0), ("0", "X01", 0), ("1", "X01", 2048), ("2", "X2", 0))):
        index(tag, third("b0", c), third("AC", c), third("WC", c))
        look(tag, xn, base)
        selfsum(xn, base, c, "b%d" % (4 + c))

    def partner(r, t):
        return (r + 1 + t % 3) % N

    def asker(t):
        return (rank - 1 - t % 3) % N

    def kpart(t):
        c = t & 3
        tt(B("KS"), cls("WIN", c), cls("VR", c), OP.add)
        ts(B("KT"), B("KS"), 13.0 * t - 1.0, OP.add)
        ts(B("KI"), B("KT"), 127, OP.bitwise_and)
        ts(third("SM", 2 * t + 1), B("KI"), col(8), OP.mult, col(3), OP.add)
        act(B("KB"), third("SM", 2 * t + 1))

    def marks(t, ms, kb):
        for m in ms:
            cm = (t + 1 + m) & 3
            mm(third("b0", m), third("S32", m), kb, True, False)
            mm(third("b0", m), third("EQ", cm), kb, False, True)
            mm(third("b1", m), third("S148", m), kb, True, False)
            mm(third("b1", m), third("EW", cm), kb, False, True)

    def spread(t, kb):
        for m in range(3):
            mm(third("b2", m), third("SEL", m), kb)
        mm(B("b3", 0, 384), kb, B("SEL"), True, False)
        for m in range(3):
            mm(third("b3", m), B("IDN"), B("BIAS"), False, m == 2)
        act(B("KM"), B("b3", 0, 384), AF.Relu)
        act(B("KRB", 0, 256), B("b2", 0, 256))
        act(B("KRB", 256, 384), B("b2", 256, 384))
        for m in range(3):
            mm(B("b3", 384 + m * 8, 392 + m * 8), third("KM", m), B("GS"))
        mm(B("b3", 416, 432), kb, B("QS", 0, 16))
        copy(B("LF"), B("b3", 384, 408))
        ts(eight("LS", t), eight("LF", 2), 128.0 + 128 * ((t + 3) & 3), OP.add)
        for m in range(2):
            ts(eight("VL", m), eight("LF", m), 128.0 + 128 * ((t + 1 + m) & 3), OP.add)
        tt(B("ZB"), B("b3", 416, 432), B("ZC", 16 * (t & 3), 16 * (t & 3) + 16), OP.add)

    def firsts():
        for c in range(8):
            for m in range(3):
                o = c * 384 + m * 128
                ts(B("EB", o, o + 128), third("KRB", m), B("LF", m * 8 + c, m * 8 + c + 1), OP.is_equal)
            mm(B("b7", 0, 384), third("WT", c), B("EB", c * 384, c * 384 + 384), c == 0, c == 7)
        for m in range(3):
            tt(third("NF", m), third("b7", m), B("TH"), OP.is_gt)

    def vj(m):
        gat("sv", third("VJ", m), B("VR", 0, 640), eight("VL", m))

    def verdict(m, xn, base):
        bank = "b%d" % (4 + m)
        o = B(bank, 0, 128)
        mm(o, third("VJ", m), B("NEGV"), True, False)
        if m < 2:
            mm(o, third("NF", m), B("BIGN"), False, False)
        for x in range(16):
            mm((T[bank][:, x:128:16], bank, 0, 128), (T[xn][:, base + x:base + 2048:16], xn, base, base + 2048), B("GS"), False, x == 15)
        act(third("CM", m), o, AF.Sign, 1.0, -0.5)
        scan(third("CN", m), B("RST", 0, 128), third("CM", m), OP.mult, OP.add)
        return (T.CN[:, m * 128 + 15:m * 128 + 128:16], "CN", m * 128, m * 128 + 128)

    def late(t):
        o = t * 144
        x2 = (t & 1) * 2048
        arrive("WL", o, o + 144, "w%d" % t, width(asker(t)))
        ts(B("LXb"), B("WL", o + 136, o + 144), -4096.0, OP.add, 2047.0, OP.min)
        tt(B("D3"), B("WL", o + 128, o + 136), eight("LQ", t), OP.min)
        copy(B("LST2"), B("D3"))
        gat("sv", B("NXb"), B("X2", x2, x2 + 2048), B("LXb"))
        mm(B("b6", 384, 512), B("BO"), B("NXb"))
        act(B("NVb"), B("b6", 384, 512))
        scamul(B("WIN", 0, 640), B("LST2"), third("S21", t & 1), B("WL", o, o + 128))
        sca(B("VR", 0, 640), B("LST2"), B("NVb"))

    def selflook(t):
        c = t & 3
        index("S", B("NU"), third("AC", c), third("WC", c))
        look("S", "XS", 0)
        selfsum("XS", 0, c, "b4")

    for t in range(RO):
        q = partner(rank, t)
        ask = asker(t)
        old = cls("WIN", t & 3)
        S = B("WIN", 640, 768)
        sm, smk = third("SM", 2 * t), third("SM", 2 * t + 1)
        lm, lk = third("LM", 2 * t), third("LM", 2 * t + 1)
        act(sm, old, AF.Identity, col(4), -1.0)
        si = B("SI")
        if t == 0:
            si = third("CS", RO)
            tt(si, sm, third("PL", 0), OP.add)
            send(q, lm, si, "m0")
        kpart(t)
        if t == 0:
            send(q, lk, smk, "k0")
        else:
            send(q, B("LM", t * 256, t * 256 + 256), B("SM", t * 256, t * 256 + 256), "m%d" % t)
        spread(t, B("KB"))
        send(q, eight("LQ", t), eight("LS", t), "f%d" % t)
        marks(t, [0, 1], B("KB"))
        mm(B("b5", 256, 384), B("DIF"), old)
        vj(0)
        firsts()
        mm(B("b3", 432, 440), third("NF", 2), B("NSEL"))
        if t:
            selflook(t - 1)
        wk = width(ask)
        if t == 0:
            arrive("LM", 0, 128, "m0", wk)
            arrive("LM", 128, 256, "k0", wk)
        else:
            arrive("LM", t * 256, t * 256 + 256, "m%d" % t, wk)
        act(B("KB2"), lk)
        marks(t, [2], B("KB2"))
        if t == 0:
            S2 = lm
        else:
            pr = (ask - 1) % N
            if pr == rank:
                pq = third("PS", t - 1)
            else:
                arrive("PQ", t * 128, t * 128 + 128, "q%d" % t, width(pr) // 2)
                pq = third("PQ", t)
            S2 = B("S2")
            tt(S2, lm, pq, OP.add)
        x2 = (t & 1) * 2048
        index("2", S2, third("b0", 2), third("b1", 2))
        look("2", "X2", x2)
        act(third("S21", t & 1), S2, AF.Identity, 1.0, 1.0)
        if t:
            solo = partner(rank, t) == (rank - 1) % N
            arrive("PL", t * 128, t * 128 + 128, "p%d" % t, width((rank - 1) % N) // (1 if solo else 2))
            tt(si, sm, third("PL", t), OP.add)
        act(S, si, AF.Identity, 1.0, 1.0)
        act(B("S1"), si, AF.Identity, 1.0, 1.0)
        index("0", si, third("b0", 0), third("b1", 0))
        look("0", "X01", 0)
        arrive("LQ", t * 8, t * 8 + 8, "f%d" % t, wk)
        copy(eight("VL", 2), eight("LQ", t))
        vj(2)
        cs = third("CS", t)
        gat("sv", cs, B("WIN", 0, 640), eight("VL", 2))
        send(ask, B("WIN", 768, 896), cs, "c%d" % t)
        e2 = verdict(2, "X2", x2)
        zs = eight("ZS", t)
        ts(zs, e2, col(10), OP.add)
        send(ask, eight("ZL", t), zs, "z%d" % t)
        index("1", si, third("b0", 1), third("b1", 1))
        look("1", "X01", 2048)
        if t:
            late(t - 1)
        vj(1)
        e0 = verdict(0, "X01", 0)
        tt(eight("Z", 0), e0, eight("ZB", 0), OP.add)
        e1 = verdict(1, "X01", 2048)
        tt(eight("Z", 1), e1, eight("ZB", 1), OP.add)
        tt(eight("Z", 2), eight("Z", 0), eight("Z", 1), OP.max)
        ts(eight("Z", 3), eight("Z", 2), col(11), OP.max)
        mm(B("b1", 384, 512), B("POLD"), old, True, False)
        arrive("ZL", t * 8, t * 8 + 8, "z%d" % t, width(q))
        zq, zx, zm = B("ZQ"), B("ZX"), B("ZM")
        wo = t * 144
        keep = B("WS", wo, wo + 128)
        tt(B("ZN"), eight("ZL", t), B("b3", 432, 440), OP.add)
        tt(zq, eight("Z", 3), B("ZN"), OP.max)
        gat("s", zx, zq, B("EXL"))
        op("v", [zm], [zq, B("EXL"), B("MSK")], lambda e: V.tensor_tensor(T.ZM[:], T.ZQ[:].indirect(T.EXL[:]), T.MSK[:], OP.mult),
           0.06 + 128 * CYC * GAT)
        mm(B("b2", 0, 128), zx, B("IDN"))
        mm(B("b3", 440, 448), zm, B("BLK"))
        ts(keep, B("b2", 0, 128), col(9), OP.is_lt)
        ts(B("ZI", 0, 8), B("b3", 440, 448), 4096.0, OP.mult, 65536.0, OP.add)
        tt(B("PP"), B("b5", 256, 384), keep, OP.mult)
        mm(B("b1", 384, 512), B("PSEL"), B("PP"), False, True)
        ps = third("PS", t)
        act(ps, B("b1", 384, 512))
        nx = (rank + 1) % N
        z = partner(nx, t + 1)
        pl = third("PL", t + 1)
        if t == RO - 1 or z == rank:
            send(nx, pl, ps, "p%d" % (t + 1))
        else:
            tr = []
            for k, (dst, land, sm_) in enumerate(((nx, pl, "p"), (z, third("PQ", t + 1), "q"))):
                en = topo.engines(core, T.cores[dst])
                en = en[k * len(en) // 2:(k + 1) * len(en) // 2]
                rid, pid = addr(dst)
                tr.append(RemoteDMATransfer(dst_ids=[DstId(rid=rid, pnc=pid)], dma_engine_mask=sum(1 << e for e in en),
                                            remote_sem=T.sem["%s%d" % (sm_, t + 1)], srcs=[ps[0]], dsts=[land[0]]))
                sent[0] += len(en)
            sends["p%d" % (t + 1)] = sends["q%d" % (t + 1)] = op(
                "g", [], [ps], lambda tr=tr: g.remote_dma_fused(tr, local_sem=T.sem["snd"]), ISSUE + LAT, "rem")
        ts(B("ZI", 32, 40), B("ZI", 0, 8), 1023, OP.bitwise_and)
        copy(B("LST"), B("ZI", 32, 40))
        ts(B("ZI", 8, 16), B("ZI", 0, 8), 13, OP.logical_shift_right)
        ts(B("ZI", 16, 24), B("ZI", 0, 8), 6144, OP.bitwise_and)
        tt(B("ZI", 8, 16), B("ZI", 8, 16), B("ZI", 16, 24), OP.add)
        lx = B("WS", wo + 136, wo + 144)
        tt(lx, B("CX"), B("ZI", 8, 16), OP.subtract)
        ts(B("LX"), lx, 4095.0, OP.min)
        gat("sv", B("NX"), B("X01"), B("LX"))
        mm(B("b7", 384, 512), B("BO"), B("NX"))
        act(B("NV"), B("b7", 384, 512))
        ws = B("WS", wo + 128, wo + 136)
        ts(ws, B("ZI", 32, 40), 768.0, OP.is_ge, 2000.0, OP.mult)
        tt(ws, ws, B("IL"), OP.max)
        send(q, B("WL", wo, wo + 144), B("WS", wo, wo + 144), "w%d" % t)
        arrive("WIN", 768, 896, "c%d" % t, width(q))
        nu, w, ls = B("NU"), B("WIN"), B("LST")
        op("sv", [nu], [w, ls], lambda e: V.tensor_scalar(T.NU[:], T.WIN[:].indirect(T.LST[:]), -1.0, None, OP.add) if e == "v"
           else S_.activation(T.NU[:], T.WIN[:].indirect(T.LST[:]), AF.Identity, bias=-1.0), 0.06 + 128 * CYC * GAT)
        scamul(w, ls, B("S1"), keep)
        sca(B("VR"), ls, B("NV"))
        act(old, nu, AF.Identity, 1.0, 1.0)

    late(RO - 1)
    for k in range(4):
        mm(third("b0", k), B("REV"), cls("WIN", k))
        ts((T.OUTB[:, k::4], "OUTB", 0, 512), third("b0", k), -1.0, OP.add)
    dma("y", [], [B("OUTB")], T.yb[:], T.OUTB[:], "o0")
    selflook(RO - 1)
    for k in range(4):
        copy((T.OUTV[:, k::4], "OUTV", 0, 512), cls("VR", k))
    dma("y", [], [B("OUTV")], T.yv[:], T.OUTV[0:128:16, :], "o1")
    arrive("PL", RO * 128, RO * 128 + 128, "p%d" % RO, width((rank - 1) % N))
    ts(B("OUTP"), third("PL", RO), -1.0, OP.add)
    dma("y", [], [B("OUTP")], T.yp[:], T.OUTP[0:128:16, :], "o2")
    flush()
    for k in ("o0", "o1", "o2"):
        g.sync.wait_ge(T.sem[k], 16)
    for k in ("cv", "cs", "ct", "cg"):
        if cnt.get(k):
            g.wait_ge(T.sem[k], cnt[k])
    g.wait_ge(T.sem["snd"], sent[0])
